import numpy as np
import ml_dtypes


def mxq(x, axis, fmt="e4m3"):
    dtype, down = {"e4m3": (ml_dtypes.float8_e4m3fn, 7), "e5m2": (ml_dtypes.float8_e5m2, 14)}[fmt]
    v = np.moveaxis(np.asarray(x, np.float32).astype(ml_dtypes.bfloat16).astype(np.float64), axis, -1)
    blocks = v.reshape(v.shape[:-1] + (-1, 32))
    amax = np.abs(blocks).max(-1, keepdims=True)
    byte = np.maximum(np.where(amax > 0, np.frexp(amax)[1] - 1 + 127, 0) - down, 1)
    scale = np.exp2(byte - 127.0)
    codes = (blocks / scale).astype(np.float32).astype(dtype).astype(np.float64)
    return np.moveaxis((codes * scale).reshape(v.shape), -1, axis)


WIDE = False


def mx_kscale(k):
    if not WIDE:
        return np.ones(k)
    levels = np.array([10, -10, 5, -5, 0])
    if k % 512:
        return np.exp2(np.random.permutation(np.resize(levels, k // 32))).repeat(32)
    a = np.empty((k // 512, 16))
    for p in range(k // 512):
        a[p, :8] = np.random.permutation(np.resize(levels, 8))
        for g in range(8):
            far = levels[np.abs(levels - a[p, g]) >= 10]
            a[p, g + 8] = far[np.random.randint(len(far))]
    return np.exp2(a.ravel()).repeat(32)


def f64(x):
    return np.asarray(x).astype(np.float64)


def striped(idx):
    return np.tile(np.asarray(idx).reshape(-1, 16).T, (8, 1)).astype(np.uint16)


def unstriped(offs):
    return offs[:16].T.reshape(-1).astype(np.int64)


def striped8(idx):
    return np.asarray(idx).reshape(8, -1, 16).transpose(0, 2, 1).reshape(128, -1).astype(np.uint16)


def unstriped8(offs):
    return offs.reshape(8, 16, -1).transpose(0, 2, 1).reshape(8, -1).astype(np.int64)


def pick8(x, idx, run):
    r = np.arange(len(x))
    return x[r[:, None], idx[r % (8 * run) // run]]


def bf(x):
    return np.asarray(x, np.float32).astype(ml_dtypes.bfloat16)


def planes(Y):
    r, m = Y.shape
    b = f64(bf(Y)).reshape(r // 32, 32, m)
    amax = np.abs(b).max(1)
    byte = np.clip(np.where(amax > 0, np.frexp(amax)[1] - 1 + 127 - 7, 1), 1, 254)
    codes = (b * np.exp2(127.0 - byte)[:, None, :]).reshape(r, m).astype(np.float32).astype(ml_dtypes.float8_e4m3fn).view(np.uint8)
    words = codes.reshape(r // 512, 128, 4, m).transpose(0, 1, 3, 2)
    return np.ascontiguousarray(words), np.ascontiguousarray(byte.astype(np.uint8).reshape(r // 512, 16, m))


D, T, U, I, Q, E = 512, 1024, 1024, 512, 256, 512


def setup_inputs():
    n = np.random.standard_normal
    idx = np.stack([np.random.permutation(T)[:I] for _ in range(8)])
    idx2 = np.random.permutation(U)[:I]
    fd = mx_kscale(D)
    fi = mx_kscale(I)
    ti = np.ones(U)
    ti[idx2] = fi
    return {
        "query": (n((D, Q)) * 0.25 / np.sqrt(D) * fd[:, None]).astype(np.float32),
        "keys": (n((D, T)) / fd[:, None]).astype(np.float32),
        "bkeys": (n((D, U)) * 0.7 / fd[:, None]).astype(np.float32),
        "size": (np.random.uniform(0.5, 2.0, (1, I)) * fi).astype(np.float32),
        "vals": (n((E, U)) / ti).astype(np.float32),
        "offs": striped8(idx),
        "offs2": striped(idx2),
    }


def reference(query, keys, bkeys, size, vals, offs, offs2):
    idx = unstriped8(offs)
    idx2 = unstriped(offs2)
    km = pick8(f64(keys), idx, 64) + f64(bkeys)[:, idx2]
    queryq = mxq(f64(query), 0, "e4m3")
    kmq = mxq(km, 0, "e4m3")
    a = queryq.T @ kmq
    p = np.exp(a - np.max(a, axis=1, keepdims=True))
    w = p * f64(size) / np.sum(p, axis=1, keepdims=True)
    wt = w.T
    vt = f64(vals)[:, idx2].T
    vtq = mxq(vt, 0, "e4m3")
    wtq = mxq(wt, 0, "e4m3")
    o = vtq.T @ wtq
    words, scales = planes(o)
    return o, words, scales

@@ -1,0 +1,234 @@
+from contextlib import ExitStack
+
+import concourse.mybir as mybir
+from concourse.masks import make_identity
+
+D, T, U, I, Q, E = 512, 1024, 1024, 512, 256, 512
+FLOPS = 2 * D * I * Q + 2 * I * E * Q
+
+F32 = mybir.dt.float32
+BF16 = mybir.dt.bfloat16
+I32 = mybir.dt.int32
+U32 = mybir.dt.uint32
+U16 = mybir.dt.uint16
+U8 = mybir.dt.uint8
+FP8X4 = mybir.dt.float8_e4m3fn_x4
+ACT = mybir.ActivationFunctionType
+ALU = mybir.AluOpType
+AXIS_X = mybir.AxisListType.X
+
+P = 128
+PACK = 4
+HALF = I // 2
+LIST_COLS = I // 16
+Q_TILES = Q // P
+
+
+def tile_attend_compositeslots_pl_kernel(tc, query, keys, bkeys, size, vals, offs, offs2, out_0, out_1, out_2):
+    nc = tc.nc
+
+    with ExitStack() as ctx:
+        sb = ctx.enter_context(tc.tile_pool(name="sb", bufs=1))
+        ps = ctx.enter_context(tc.psum_pool(name="ps", bufs=1))
+
+        def sbuf(name, shape, dtype, tag=None):
+            return sb.tile(shape, dtype, name=name, tag=tag or name, align_bytes=64)
+
+        def quantise(name, grouped, width, tag=None):
+            codes = sbuf(name + "_codes", [P, width], U32, tag)
+            scales = sbuf(name + "_scales", [P, width], U8)
+            nc.vector.quantize_mx(out=codes[:].bitcast(FP8X4), scales=scales[:], in_=grouped[:].rearrange("p c t -> p (c t)"))
+            return codes, scales
+
+        def half_of(lists, h):
+            return lists[:, h * LIST_COLS // 2 : (h + 1) * LIST_COLS // 2]
+
+        def interleave(copy, grouped, first, planes):
+            count = planes.shape[1]
+            copy(
+                grouped[:, :, first : first + count].rearrange("p (c i) t -> p c t i", i=4),
+                planes.rearrange("p t (c i) -> p c t i", i=4),
+            )
+
+        size_sb = sbuf("size_sb", [P, PACK], F32)
+        nc.sync.dma_start(size_sb[:], size.rearrange("o (p t) -> p (o t)", t=PACK))
+        query_sb = sbuf("query_sb", [P, PACK, Q], F32)
+        nc.sync.dma_start(query_sb[:], query.rearrange("(p t) q -> p t q", t=PACK))
+        own_lists = sbuf("own_lists", [P, LIST_COLS], U16)
+        shared_list = sbuf("shared_list", [P, LIST_COLS], U16)
+
+        def load_plane(name, table, t):
+            plane = sbuf(name + str(t), [P, table.shape[1]], F32)
+            nc.sync.dma_start(plane[:], table.rearrange("(p t) n -> p t n", t=PACK)[:, t, :])
+            return plane
+
+        base_planes, key_planes = [], []
+        for t in range(PACK):
+            base_planes.append(load_plane("base_plane", bkeys, t))
+            if t == 0:
+                nc.sync.dma_start(shared_list[:], offs2)
+                nc.sync.dma_start(own_lists[:], offs)
+            key_planes.append(load_plane("key_plane", keys, t))
+        val_planes = [load_plane("val_plane", vals, j) for j in range(PACK)]
+
+        ident = sbuf("ident", [P, P], F32)
+        make_identity(nc, ident[:])
+
+        query_grouped = sbuf("query_grouped", [P, Q, PACK], BF16)
+        interleave(nc.vector.tensor_copy, query_grouped, 0, query_sb[:])
+        query_codes, query_scales = quantise("query", query_grouped, Q)
+
+        size_bank = ps.tile([P, PACK, P], F32, name="size_bank", tag="bank_size")
+        for t in range(PACK):
+            nc.tensor.transpose(size_bank[:, t, :], size_sb[:, t : t + 1].to_broadcast([P, P]), ident[:])
+        size_row = sbuf("size_row", [P, I], F32)
+        nc.scalar.copy(size_row[:].rearrange("p (s t) -> p s t", t=PACK), size_bank[:].rearrange("p t s -> p s t"))
+
+        base_picked = [sbuf("base_picked%d" % t, [P, I], F32) for t in range(PACK)]
+        km_low = sbuf("km_low", [P, 2, I], F32)
+        km_high = [sbuf("km_high%d" % h, [P, 2, HALF], F32) for h in range(2)]
+        km_grouped = [sbuf("km_grouped%d" % h, [P, HALF, PACK], BF16) for h in range(2)]
+
+        def gather_add(out, t, offsets, cols):
+            nc.vector.tensor_tensor(out, key_planes[t][:].indirect(offsets), base_picked[t][:, cols], ALU.add)
+
+        halves = [slice(0, HALF), slice(HALF, I)]
+        for t in range(PACK):
+            if t < PACK - 1:
+                nc.scalar.activation(base_picked[t][:], base_planes[t][:].indirect(shared_list[:]), ACT.Copy)
+            else:
+                for h in range(2):
+                    nc.scalar.activation(base_picked[t][:, halves[h]], base_planes[t][:].indirect(half_of(shared_list, h)), ACT.Copy)
+            if t < 2:
+                gather_add(km_low[:, t, :], t, own_lists[:], slice(0, I))
+            if t == 1:
+                for h in range(2):
+                    interleave(nc.vector.tensor_copy, km_grouped[h], 0, km_low[:, :, halves[h]])
+            if t == 2:
+                for h in range(2):
+                    gather_add(km_high[h][:, 0, :], t, half_of(own_lists, h), halves[h])
+        last = PACK - 1
+        key_picked = sbuf("key_picked", [P, HALF], F32)
+        gather_add(km_high[0][:, 1, :], last, half_of(own_lists, 0), halves[0])
+        nc.scalar.activation(key_picked[:], key_planes[last][:].indirect(half_of(own_lists, 1)), ACT.Copy)
+        nc.vector.tensor_tensor(km_high[1][:, 1, :], key_picked[:], base_picked[last][:, halves[1]], ALU.add)
+        interleave(nc.scalar.copy, km_grouped[0], 2, km_high[0][:])
+        interleave(nc.vector.tensor_copy, km_grouped[1], 2, km_high[1][:])
+
+        score_banks = [ps.tile([P, I], F32, name="score_bank", tag="bank_score%d" % a) for a in range(Q_TILES)]
+        for h in range(2):
+            km_codes, km_scales = quantise("km%d" % h, km_grouped[h], HALF)
+            for a in range(Q_TILES):
+                rows = slice(a * P, (a + 1) * P)
+                nc.tensor.matmul_mx(
+                    out=score_banks[a][:, halves[h]],
+                    lhsT=query_codes[:, rows].bitcast(FP8X4),
+                    lhsT_scale=query_scales[:, rows],
+                    rhs=km_codes[:].bitcast(FP8X4),
+                    rhs_scale=km_scales[:],
+                    start=True,
+                    stop=True,
+                )
+
+        def turn(rows_bf16, bank):
+            words = rows_bf16[:].bitcast(F32)
+            for u in range(2):
+                nc.tensor.transpose(bank[:, u, :], words[:, u : I // 2 : 2], ident[:])
+
+        def as_word_pairs(grouped):
+            return grouped.rearrange("p c t -> p (c t)").bitcast(F32).rearrange("p (c u) -> p c u", u=2)
+
+        val_picked = [sbuf("val_picked%d" % j, [P, I], BF16) for j in range(PACK)]
+
+        def gather_vals_scalar(j, cols, offsets):
+            nc.scalar.activation(val_picked[j][:, cols], val_planes[j][:].indirect(offsets), ACT.Copy)
+
+        def gather_vals_vector(j, cols, offsets):
+            nc.vector.tensor_copy(val_picked[j][:, cols], val_planes[j][:].indirect(offsets))
+
+        gather_vals_scalar(0, slice(0, I), shared_list[:])
+        gather_vals_vector(1, halves[0], half_of(shared_list, 0))
+        gather_vals_scalar(1, halves[1], half_of(shared_list, 1))
+
+        neg_max = [sbuf("neg_max0", [P, 1], F32)[:], val_picked[2][:, HALF : HALF + 2].bitcast(F32)]
+        inv_sum = [sbuf("inv_sum0", [P, 1], F32)[:], val_picked[3][:, 0:2].bitcast(F32)]
+        row_sum = [sbuf("row_sum%d" % a, [P, 1], F32) for a in range(Q_TILES)]
+        probs = [sbuf("probs%d" % a, [P, I], F32) for a in range(Q_TILES)]
+        weights = [sbuf("weights%d" % a, [P, I], BF16) for a in range(Q_TILES)]
+        for a in range(Q_TILES):
+            nc.vector.tensor_reduce(neg_max[a], score_banks[a][:], AXIS_X, ALU.max, negate=True)
+        for a in range(Q_TILES):
+            nc.scalar.activation(probs[a][:], score_banks[a][:], ACT.Exp, bias=neg_max[a], accum_out=row_sum[a][:])
+        gather_vals_vector(2, halves[0], half_of(shared_list, 0))
+        for a in range(Q_TILES):
+            nc.vector.reciprocal(inv_sum[a], row_sum[a][:])
+            nc.vector.scalar_tensor_tensor(weights[a][:], probs[a][:], inv_sum[a], size_row[:], ALU.mult, ALU.mult)
+        gather_vals_scalar(2, halves[1], half_of(shared_list, 1))
+        gather_vals_scalar(3, halves[1], half_of(shared_list, 1))
+        gather_vals_vector(3, halves[0], half_of(shared_list, 0))
+
+        weight_codes = sbuf("weight_codes", [P, Q], U32)
+        weight_scales = sbuf("weight_scales", [P, Q], U8)
+        val_grouped, val_mx, weight_grouped = {}, {}, {}
+
+        def turn_vals(j, copy, bank_tag, tag=None):
+            bank = ps.tile([P, 2, P], F32, name="val_bank", tag=bank_tag)
+            turn(val_picked[j], bank)
+            val_grouped[j] = sbuf("val_grouped%d" % j, [P, P, PACK], BF16, tag)
+            copy(as_word_pairs(val_grouped[j][:]), bank[:].rearrange("p u c -> p c u"))
+
+        def turn_weights(a):
+            bank = ps.tile([P, 2, P], F32, name="weight_bank", tag="bank_weight%d" % a)
+            turn(weights[a], bank)
+            weight_grouped[a] = sbuf("weight_grouped%d" % a, [P, P, PACK], BF16)
+            nc.scalar.copy(as_word_pairs(weight_grouped[a][:]), bank[:].rearrange("p u c -> p c u"))
+
+        def quantise_weights(a):
+            cols = slice(a * P, (a + 1) * P)
+            nc.vector.quantize_mx(
+                out=weight_codes[:, cols].bitcast(FP8X4),
+                scales=weight_scales[:, cols],
+                in_=weight_grouped[a][:].rearrange("p c t -> p (c t)"),
+            )
+
+        turn_vals(0, nc.scalar.copy, "bank_score0")
+        val_mx[0] = quantise("val0", val_grouped[0], P, "probs0")
+        turn_weights(0)
+        turn_weights(1)
+        turn_vals(2, nc.vector.tensor_copy, "bank_val2", "probs1")
+        quantise_weights(0)
+        val_mx[2] = quantise("val2", val_grouped[2], P)
+        quantise_weights(1)
+        turn_vals(1, nc.scalar.copy, "bank_weight0")
+        turn_vals(3, nc.scalar.copy, "bank_val3")
+        val_mx[1] = quantise("val1", val_grouped[1], P)
+        val_mx[3] = quantise("val3", val_grouped[3], P)
+
+        out_rows = out_0.rearrange("(p j) q -> p j q", j=PACK)
+        result_grouped = sbuf("result_grouped", [P, Q, PACK], BF16)
+        out_tags = ("bank_size", "bank_out1", "bank_score1", "bank_score0")
+        results = [sbuf("result%d" % pair, [P, 2, Q], F32) for pair in range(2)]
+        for j in range(PACK):
+            bank = ps.tile([P, Q], F32, name="out_bank", tag=out_tags[j])
+            nc.tensor.matmul_mx(
+                out=bank[:],
+                lhsT=val_mx[j][0][:].bitcast(FP8X4),
+                lhsT_scale=val_mx[j][1][:],
+                rhs=weight_codes[:].bitcast(FP8X4),
+                rhs_scale=weight_scales[:],
+                start=True,
+                stop=True,
+            )
+            copy = nc.vector.tensor_copy if j == 1 else nc.scalar.copy
+            copy(results[j // 2][:, j % 2, :], bank[:])
+        for pair in range(2):
+            nc.sync.dma_start(out_rows[:, 2 * pair : 2 * pair + 2, :], results[pair][:])
+            interleave(nc.vector.tensor_copy, result_grouped, 2 * pair, results[pair][:])
+        out_codes, out_scales = quantise("out", result_grouped, Q)
+        nc.sync.dma_start(out_1[0].rearrange("p c r -> p (c r)").bitcast(I32), out_codes[:].bitcast(I32))
+        for quad in range(4):
+            queue = nc.sync if quad % 2 else nc.scalar
+            queue.dma_start(
+                out_2[0, 4 * quad : 4 * quad + 4, :].bitcast(I32),
+                out_scales[32 * quad : 32 * quad + 4, :].bitcast(I32),
+            )

@@ -79,26 +79,29 @@ def tile_attend_compositeslots_pl_kernel(tc, query, keys, bkeys, size, vals, off
         query_codes, query_scales = quantise("query", query_grouped, Q)
 
         size_bank = ps.tile([P, PACK, P], F32, name="size_bank", tag="bank_size")
+        size_spread = sbuf("size_spread", [P, PACK, P], F32)
+        nc.scalar.activation(size_spread[:], size_sb[:].unsqueeze(2).to_broadcast([P, PACK, P]), ACT.Copy)
         for t in range(PACK):
-            nc.tensor.transpose(size_bank[:, t, :], size_sb[:, t : t + 1].to_broadcast([P, P]), ident[:])
+            nc.tensor.transpose(size_bank[:, t, :], size_spread[:, t, :], ident[:])
         size_row = sbuf("size_row", [P, I], F32)
-        nc.scalar.copy(size_row[:].rearrange("p (s t) -> p s t", t=PACK), size_bank[:].rearrange("p t s -> p s t"))
+        nc.vector.tensor_copy(size_row[:].rearrange("p (u s e) -> p u s e", u=2, e=2), size_bank[:].rearrange("p (u e) s -> p u s e", u=2))
 
         base_picked = [sbuf("base_picked%d" % t, [P, I], F32) for t in range(PACK)]
         km_low = sbuf("km_low", [P, 2, I], F32)
         km_high = [sbuf("km_high%d" % h, [P, 2, HALF], F32) for h in range(2)]
-        km_grouped = [sbuf("km_grouped%d" % h, [P, HALF, PACK], BF16) for h in range(2)]
+        shared_bytes = sbuf("shared_bytes", [P, HALF + HALF * PACK], BF16)
+        km_grouped = [
+            sbuf("km_grouped0", [P, HALF, PACK], BF16)[:],
+            shared_bytes[:, HALF:].rearrange("p (c t) -> p c t", t=PACK),
+        ]
 
         def gather_add(out, t, offsets, cols):
             nc.vector.tensor_tensor(out, key_planes[t][:].indirect(offsets), base_picked[t][:, cols], ALU.add)
 
         halves = [slice(0, HALF), slice(HALF, I)]
-        for t in range(PACK):
-            if t < PACK - 1:
-                nc.scalar.activation(base_picked[t][:], base_planes[t][:].indirect(shared_list[:]), ACT.Copy)
-            else:
-                for h in range(2):
-                    nc.scalar.activation(base_picked[t][:, halves[h]], base_planes[t][:].indirect(half_of(shared_list, h)), ACT.Copy)
+        last = PACK - 1
+        for t in range(last):
+            nc.scalar.activation(base_picked[t][:], base_planes[t][:].indirect(shared_list[:]), ACT.Copy)
             if t < 2:
                 gather_add(km_low[:, t, :], t, own_lists[:], slice(0, I))
             if t == 1:
@@ -107,7 +110,8 @@ def tile_attend_compositeslots_pl_kernel(tc, query, keys, bkeys, size, vals, off
             if t == 2:
                 for h in range(2):
                     gather_add(km_high[h][:, 0, :], t, half_of(own_lists, h), halves[h])
-        last = PACK - 1
+        nc.scalar.activation(base_picked[last][:, halves[0]], base_planes[last][:].indirect(half_of(shared_list, 0)), ACT.Copy)
+        nc.vector.tensor_copy(base_picked[last][:, halves[1]], base_planes[last][:].indirect(half_of(shared_list, 1)))
         key_picked = sbuf("key_picked", [P, HALF], F32)
         gather_add(km_high[0][:, 1, :], last, half_of(own_lists, 0), halves[0])
         nc.scalar.activation(key_picked[:], key_planes[last][:].indirect(half_of(own_lists, 1)), ACT.Copy)
@@ -116,29 +120,34 @@ def tile_attend_compositeslots_pl_kernel(tc, query, keys, bkeys, size, vals, off
         interleave(nc.vector.tensor_copy, km_grouped[1], 2, km_high[1][:])
 
         score_banks = [ps.tile([P, I], F32, name="score_bank", tag="bank_score%d" % a) for a in range(Q_TILES)]
-        for h in range(2):
-            km_codes, km_scales = quantise("km%d" % h, km_grouped[h], HALF)
-            for a in range(Q_TILES):
-                rows = slice(a * P, (a + 1) * P)
-                nc.tensor.matmul_mx(
-                    out=score_banks[a][:, halves[h]],
-                    lhsT=query_codes[:, rows].bitcast(FP8X4),
-                    lhsT_scale=query_scales[:, rows],
-                    rhs=km_codes[:].bitcast(FP8X4),
-                    rhs_scale=km_scales[:],
-                    start=True,
-                    stop=True,
-                )
+        km_codes = sbuf("km_codes", [P, I], U32)
+        km_scales = sbuf("km_scales", [P, I], U8)
 
-        def turn(rows_bf16, bank):
-            words = rows_bf16[:].bitcast(F32)
-            for u in range(2):
-                nc.tensor.transpose(bank[:, u, :], words[:, u : I // 2 : 2], ident[:])
+        def scores(a, slots):
+            rows = slice(a * P, (a + 1) * P)
+            nc.tensor.matmul_mx(
+                out=score_banks[a][:, slots],
+                lhsT=query_codes[:, rows].bitcast(FP8X4),
+                lhsT_scale=query_scales[:, rows],
+                rhs=km_codes[:, slots].bitcast(FP8X4),
+                rhs_scale=km_scales[:, slots],
+                start=True,
+                stop=True,
+            )
+
+        for h in range(2):
+            nc.vector.quantize_mx(
+                out=km_codes[:, halves[h]].bitcast(FP8X4),
+                scales=km_scales[:, halves[h]],
+                in_=km_grouped[h].rearrange("p c t -> p (c t)"),
+            )
+            scores(0, halves[h])
+        scores(1, slice(0, I))
 
         def as_word_pairs(grouped):
             return grouped.rearrange("p c t -> p (c t)").bitcast(F32).rearrange("p (c u) -> p c u", u=2)
 
-        val_picked = [sbuf("val_picked%d" % j, [P, I], BF16) for j in range(PACK)]
+        val_picked = {0: shared_bytes[:, 0:I], 1: sbuf("val_picked1", [P, I], BF16)[:], 2: sbuf("val_picked2", [P, I], BF16)[:]}
 
         def gather_vals_scalar(j, cols, offsets):
             nc.scalar.activation(val_picked[j][:, cols], val_planes[j][:].indirect(offsets), ACT.Copy)
@@ -146,42 +155,66 @@ def tile_attend_compositeslots_pl_kernel(tc, query, keys, bkeys, size, vals, off
         def gather_vals_vector(j, cols, offsets):
             nc.vector.tensor_copy(val_picked[j][:, cols], val_planes[j][:].indirect(offsets))
 
-        gather_vals_scalar(0, slice(0, I), shared_list[:])
-        gather_vals_vector(1, halves[0], half_of(shared_list, 0))
-        gather_vals_scalar(1, halves[1], half_of(shared_list, 1))
+        def slots(first, stop):
+            return slice(first, stop), shared_list[:, first // 16 : stop // 16]
 
-        neg_max = [sbuf("neg_max0", [P, 1], F32)[:], val_picked[2][:, HALF : HALF + 2].bitcast(F32)]
-        inv_sum = [sbuf("inv_sum0", [P, 1], F32)[:], val_picked[3][:, 0:2].bitcast(F32)]
-        row_sum = [sbuf("row_sum%d" % a, [P, 1], F32) for a in range(Q_TILES)]
+        val_banks = {}
+
+        def turn_vals(j, bank_tag):
+            val_banks[j] = ps.tile([P, 2, P], F32, name="val_bank", tag=bank_tag)
+            words = val_picked[j].bitcast(F32)
+            for u in range(2):
+                nc.tensor.transpose(val_banks[j][:, u, :], words[:, u : I // 2 : 2], ident[:])
+
+        gather_vals_scalar(0, halves[0], half_of(shared_list, 0))
+        gather_vals_vector(0, halves[1], half_of(shared_list, 1))
+        gather_vals_scalar(1, slice(0, I), shared_list[:])
+        gather_vals_scalar(2, *slots(P, I))
+        turn_vals(0, "bank_val0")
+        val_picked[3] = shared_bytes[:, P : P + I]
+
+        neg_max = [val_picked[2][:, 0:2].bitcast(F32), val_picked[3][:, I - 2 : I].bitcast(F32)]
+        inv_sum = sbuf("inv_sum", [P, Q_TILES], F32)
+        row_sum = sbuf("row_sum", [P, Q_TILES], F32)
         probs = [sbuf("probs%d" % a, [P, I], F32) for a in range(Q_TILES)]
         weights = [sbuf("weights%d" % a, [P, I], BF16) for a in range(Q_TILES)]
         for a in range(Q_TILES):
             nc.vector.tensor_reduce(neg_max[a], score_banks[a][:], AXIS_X, ALU.max, negate=True)
         for a in range(Q_TILES):
-            nc.scalar.activation(probs[a][:], score_banks[a][:], ACT.Exp, bias=neg_max[a], accum_out=row_sum[a][:])
-        gather_vals_vector(2, halves[0], half_of(shared_list, 0))
-        for a in range(Q_TILES):
-            nc.vector.reciprocal(inv_sum[a], row_sum[a][:])
-            nc.vector.scalar_tensor_tensor(weights[a][:], probs[a][:], inv_sum[a], size_row[:], ALU.mult, ALU.mult)
-        gather_vals_scalar(2, halves[1], half_of(shared_list, 1))
-        gather_vals_scalar(3, halves[1], half_of(shared_list, 1))
-        gather_vals_vector(3, halves[0], half_of(shared_list, 0))
+            nc.scalar.activation(
+                probs[a][:].rearrange("p (u s e) -> p u s e", u=2, e=2),
+                score_banks[a][:].rearrange("p (s u e) -> p u s e", u=2, e=2),
+                ACT.Exp,
+                bias=neg_max[a],
+                accum_out=row_sum[:, a : a + 1],
+            )
+        gather_vals_vector(3, *slots(0, I - P))
+        gather_vals_scalar(2, *slots(0, P))
+        gather_vals_scalar(3, *slots(I - P, I))
+        nc.vector.reciprocal(inv_sum[:], row_sum[:])
 
         weight_codes = sbuf("weight_codes", [P, Q], U32)
         weight_scales = sbuf("weight_scales", [P, Q], U8)
-        val_grouped, val_mx, weight_grouped = {}, {}, {}
+        val_grouped, val_mx, weight_grouped, weight_banks = {}, {}, {}, {}
 
-        def turn_vals(j, copy, bank_tag, tag=None):
-            bank = ps.tile([P, 2, P], F32, name="val_bank", tag=bank_tag)
-            turn(val_picked[j], bank)
-            val_grouped[j] = sbuf("val_grouped%d" % j, [P, P, PACK], BF16, tag)
-            copy(as_word_pairs(val_grouped[j][:]), bank[:].rearrange("p u c -> p c u"))
+        def make_weights(a):
+            weight_banks[a] = ps.tile([P, 2, P], F32, name="weight_bank", tag="bank_weight%d" % a)
+            for u in range(2):
+                nc.vector.scalar_tensor_tensor(
+                    weights[a][:, halves[u]], probs[a][:, halves[u]], inv_sum[:, a : a + 1], size_row[:, halves[u]], ALU.mult, ALU.mult
+                )
+                nc.tensor.transpose(weight_banks[a][:, u, :], weights[a][:, halves[u]].bitcast(F32), ident[:])
 
-        def turn_weights(a):
-            bank = ps.tile([P, 2, P], F32, name="weight_bank", tag="bank_weight%d" % a)
-            turn(weights[a], bank)
+        for pair, tag in enumerate(("row_sum", None)):
+            val_grouped[pair] = sbuf("val_grouped%d" % pair, [P, 2 * P, PACK], BF16, tag)
+
+        def group_vals(j):
+            cols = slice(j % 2 * P, (j % 2 + 1) * P)
+            nc.scalar.copy(as_word_pairs(val_grouped[j // 2][:, cols, :]), val_banks[j][:].rearrange("p u c -> p c u"))
+
+        def group_weights(a):
             weight_grouped[a] = sbuf("weight_grouped%d" % a, [P, P, PACK], BF16)
-            nc.scalar.copy(as_word_pairs(weight_grouped[a][:]), bank[:].rearrange("p u c -> p c u"))
+            nc.scalar.copy(as_word_pairs(weight_grouped[a][:]), weight_banks[a][:].rearrange("p u c -> p c u"))
 
         def quantise_weights(a):
             cols = slice(a * P, (a + 1) * P)
@@ -191,40 +224,49 @@ def tile_attend_compositeslots_pl_kernel(tc, query, keys, bkeys, size, vals, off
                 in_=weight_grouped[a][:].rearrange("p c t -> p (c t)"),
             )
 
-        turn_vals(0, nc.scalar.copy, "bank_score0")
-        val_mx[0] = quantise("val0", val_grouped[0], P, "probs0")
-        turn_weights(0)
-        turn_weights(1)
-        turn_vals(2, nc.vector.tensor_copy, "bank_val2", "probs1")
+        group_vals(0)
+        for j, bank_tag in ((1, "bank_score0"), (2, "bank_val2"), (3, "bank_val3")):
+            turn_vals(j, bank_tag)
+            group_vals(j)
+        for a in range(Q_TILES):
+            make_weights(a)
+            group_weights(a)
         quantise_weights(0)
-        val_mx[2] = quantise("val2", val_grouped[2], P)
+        for pair, tag in enumerate(("probs0", None)):
+            val_mx[pair] = quantise("val%d" % pair, val_grouped[pair], 2 * P, tag)
         quantise_weights(1)
-        turn_vals(1, nc.scalar.copy, "bank_weight0")
-        turn_vals(3, nc.scalar.copy, "bank_val3")
-        val_mx[1] = quantise("val1", val_grouped[1], P)
-        val_mx[3] = quantise("val3", val_grouped[3], P)
 
         out_rows = out_0.rearrange("(p j) q -> p j q", j=PACK)
-        result_grouped = sbuf("result_grouped", [P, Q, PACK], BF16)
-        out_tags = ("bank_size", "bank_out1", "bank_score1", "bank_score0")
-        results = [sbuf("result%d" % pair, [P, 2, Q], F32) for pair in range(2)]
-        for j in range(PACK):
-            bank = ps.tile([P, Q], F32, name="out_bank", tag=out_tags[j])
-            nc.tensor.matmul_mx(
-                out=bank[:],
-                lhsT=val_mx[j][0][:].bitcast(FP8X4),
-                lhsT_scale=val_mx[j][1][:],
-                rhs=weight_codes[:].bitcast(FP8X4),
-                rhs_scale=weight_scales[:],
-                start=True,
-                stop=True,
+        out_codes = sbuf("out_codes", [P, Q], U32)
+        out_scales = sbuf("out_scales", [P, Q], U8)
+        parts = (((0, PACK, "bank_size"),), ((0, 2, "bank_score0"), (2, 2, "bank_score1")))
+        for a in range(Q_TILES):
+            cols = slice(a * P, (a + 1) * P)
+            result_grouped = sbuf("result_grouped%d" % a, [P, P, PACK], BF16)
+            for first, count, bank_tag in parts[a]:
+                bank = ps.tile([P, count, P], F32, name="out_bank", tag=bank_tag)
+                for e in range(count):
+                    j = first + e
+                    codes, scales = val_mx[j // 2]
+                    features = slice(j % 2 * P, (j % 2 + 1) * P)
+                    nc.tensor.matmul_mx(
+                        out=bank[:, e, :],
+                        lhsT=codes[:, features].bitcast(FP8X4),
+                        lhsT_scale=scales[:, features],
+                        rhs=weight_codes[:, cols].bitcast(FP8X4),
+                        rhs_scale=weight_scales[:, cols],
+                        start=True,
+                        stop=True,
+                    )
+                result = sbuf("result%d_%d" % (a, first), [P, count, P], F32)
+                nc.scalar.copy(result[:], bank[:])
+                nc.sync.dma_start(out_rows[:, first : first + count, cols], result[:])
+                interleave(nc.vector.tensor_copy, result_grouped, first, result[:])
+            nc.vector.quantize_mx(
+                out=out_codes[:, cols].bitcast(FP8X4),
+                scales=out_scales[:, cols],
+                in_=result_grouped[:].rearrange("p c t -> p (c t)"),
             )
-            copy = nc.vector.tensor_copy if j == 1 else nc.scalar.copy
-            copy(results[j // 2][:, j % 2, :], bank[:])
-        for pair in range(2):
-            nc.sync.dma_start(out_rows[:, 2 * pair : 2 * pair + 2, :], results[pair][:])
-            interleave(nc.vector.tensor_copy, result_grouped, 2 * pair, results[pair][:])
-        out_codes, out_scales = quantise("out", result_grouped, Q)
         nc.sync.dma_start(out_1[0].rearrange("p c r -> p (c r)").bitcast(I32), out_codes[:].bitcast(I32))
         for quad in range(4):
             queue = nc.sync if quad % 2 else nc.scalar

@@ -147,7 +147,7 @@ def tile_attend_compositeslots_pl_kernel(tc, query, keys, bkeys, size, vals, off
         def as_word_pairs(grouped):
             return grouped.rearrange("p c t -> p (c t)").bitcast(F32).rearrange("p (c u) -> p c u", u=2)
 
-        val_picked = {0: shared_bytes[:, 0:I], 1: sbuf("val_picked1", [P, I], BF16)[:], 2: sbuf("val_picked2", [P, I], BF16)[:]}
+        val_picked = {0: shared_bytes[:, 0:I], 1: sbuf("val_picked1", [P, I], BF16)[:], 3: sbuf("val_picked3", [P, I], BF16)[:]}
 
         def gather_vals_scalar(j, cols, offsets):
             nc.scalar.activation(val_picked[j][:, cols], val_planes[j][:].indirect(offsets), ACT.Copy)
@@ -169,13 +169,13 @@ def tile_attend_compositeslots_pl_kernel(tc, query, keys, bkeys, size, vals, off
         gather_vals_scalar(0, halves[0], half_of(shared_list, 0))
         gather_vals_vector(0, halves[1], half_of(shared_list, 1))
         gather_vals_scalar(1, slice(0, I), shared_list[:])
-        gather_vals_scalar(2, *slots(P, I))
         turn_vals(0, "bank_val0")
-        val_picked[3] = shared_bytes[:, P : P + I]
+        val_picked[2] = shared_bytes[:, HALF : HALF + I]
+        gather_vals_scalar(2, *slots(HALF, I))
 
-        neg_max = [val_picked[2][:, 0:2].bitcast(F32), val_picked[3][:, I - 2 : I].bitcast(F32)]
-        inv_sum = sbuf("inv_sum", [P, Q_TILES], F32)
-        row_sum = sbuf("row_sum", [P, Q_TILES], F32)
+        neg_max = [val_picked[3][:, 0:2].bitcast(F32), val_picked[3][:, I - 2 : I].bitcast(F32)]
+        inv_sum = [sbuf("inv_sum%d" % a, [P, 1], F32) for a in range(Q_TILES)]
+        row_sum = [sbuf("row_sum%d" % a, [P, 1], F32) for a in range(Q_TILES)]
         probs = [sbuf("probs%d" % a, [P, I], F32) for a in range(Q_TILES)]
         weights = [sbuf("weights%d" % a, [P, I], BF16) for a in range(Q_TILES)]
         for a in range(Q_TILES):
@@ -186,31 +186,33 @@ def tile_attend_compositeslots_pl_kernel(tc, query, keys, bkeys, size, vals, off
                 score_banks[a][:].rearrange("p (s u e) -> p u s e", u=2, e=2),
                 ACT.Exp,
                 bias=neg_max[a],
-                accum_out=row_sum[:, a : a + 1],
+                accum_out=row_sum[a][:],
             )
-        gather_vals_vector(3, *slots(0, I - P))
-        gather_vals_scalar(2, *slots(0, P))
-        gather_vals_scalar(3, *slots(I - P, I))
-        nc.vector.reciprocal(inv_sum[:], row_sum[:])
+        gather_vals_vector(2, *slots(0, HALF))
+        gather_vals_vector(3, *slots(0, P))
+        gather_vals_scalar(3, *slots(P, I))
 
         weight_codes = sbuf("weight_codes", [P, Q], U32)
         weight_scales = sbuf("weight_scales", [P, Q], U8)
         val_grouped, val_mx, weight_grouped, weight_banks = {}, {}, {}, {}
 
-        def make_weights(a):
-            weight_banks[a] = ps.tile([P, 2, P], F32, name="weight_bank", tag="bank_weight%d" % a)
-            for u in range(2):
-                nc.vector.scalar_tensor_tensor(
-                    weights[a][:, halves[u]], probs[a][:, halves[u]], inv_sum[:, a : a + 1], size_row[:, halves[u]], ALU.mult, ALU.mult
-                )
-                nc.tensor.transpose(weight_banks[a][:, u, :], weights[a][:, halves[u]].bitcast(F32), ident[:])
+        def make_weights(a, u):
+            if a == 0:
+                sizes = size_bank[:, 2 * u : 2 * u + 2, :].rearrange("p e s -> p s e")
+            else:
+                sizes = size_row[:, halves[u]].rearrange("p (s e) -> p s e", e=2)
+            nc.vector.scalar_tensor_tensor(
+                weights[a][:, halves[u]].rearrange("p (s e) -> p s e", e=2),
+                probs[a][:, halves[u]].rearrange("p (s e) -> p s e", e=2),
+                inv_sum[a][:],
+                sizes,
+                ALU.mult,
+                ALU.mult,
+            )
+            nc.tensor.transpose(weight_banks[a][:, u, :], weights[a][:, halves[u]].bitcast(F32), ident[:])
 
-        for pair, tag in enumerate(("row_sum", None)):
-            val_grouped[pair] = sbuf("val_grouped%d" % pair, [P, 2 * P, PACK], BF16, tag)
-
-        def group_vals(j):
-            cols = slice(j % 2 * P, (j % 2 + 1) * P)
-            nc.scalar.copy(as_word_pairs(val_grouped[j // 2][:, cols, :]), val_banks[j][:].rearrange("p u c -> p c u"))
+        def group_vals(j, copy, grouped):
+            copy(as_word_pairs(grouped), val_banks[j][:].rearrange("p u c -> p c u"))
 
         def group_weights(a):
             weight_grouped[a] = sbuf("weight_grouped%d" % a, [P, P, PACK], BF16)
@@ -224,48 +226,65 @@ def tile_attend_compositeslots_pl_kernel(tc, query, keys, bkeys, size, vals, off
                 in_=weight_grouped[a][:].rearrange("p c t -> p (c t)"),
             )
 
-        group_vals(0)
-        for j, bank_tag in ((1, "bank_score0"), (2, "bank_val2"), (3, "bank_val3")):
-            turn_vals(j, bank_tag)
-            group_vals(j)
         for a in range(Q_TILES):
-            make_weights(a)
-            group_weights(a)
+            weight_banks[a] = ps.tile([P, 2, P], F32, name="weight_bank", tag="bank_weight%d" % a)
+        nc.vector.reciprocal(inv_sum[0][:], row_sum[0][:])
+        make_weights(0, 0)
+        nc.vector.reciprocal(inv_sum[1][:], row_sum[1][:])
+        make_weights(0, 1)
+        group_weights(0)
+        make_weights(1, 0)
+        make_weights(1, 1)
+        group_weights(1)
+
+        low_grouped = sbuf("val_grouped01", [P, 2 * P, PACK], BF16, "probs1")
+        group_vals(0, nc.vector.tensor_copy, low_grouped[:, 0:P, :])
+        turn_vals(1, "bank_score0")
+        group_vals(1, nc.vector.tensor_copy, low_grouped[:, P:, :])
+        for j, bank_tag, tag in ((2, "bank_val2", "row_sum1"), (3, "bank_size", None)):
+            turn_vals(j, bank_tag)
+            val_grouped[j] = sbuf("val_grouped%d" % j, [P, P, PACK], BF16, tag)
+            group_vals(j, nc.scalar.copy, val_grouped[j][:])
         quantise_weights(0)
-        for pair, tag in enumerate(("probs0", None)):
-            val_mx[pair] = quantise("val%d" % pair, val_grouped[pair], 2 * P, tag)
+        low_codes, low_scales = quantise("val01", low_grouped, 2 * P)
+        for j in range(2):
+            val_mx[j] = low_codes[:, j * P : (j + 1) * P], low_scales[:, j * P : (j + 1) * P]
+        codes, scales = quantise("val2", val_grouped[2], P, "size_row")
+        val_mx[2] = codes[:], scales[:]
         quantise_weights(1)
+        codes, scales = quantise("val3", val_grouped[3], P)
+        val_mx[3] = codes[:], scales[:]
 
         out_rows = out_0.rearrange("(p j) q -> p j q", j=PACK)
         out_codes = sbuf("out_codes", [P, Q], U32)
         out_scales = sbuf("out_scales", [P, Q], U8)
-        parts = (((0, PACK, "bank_size"),), ((0, 2, "bank_score0"), (2, 2, "bank_score1")))
-        for a in range(Q_TILES):
-            cols = slice(a * P, (a + 1) * P)
-            result_grouped = sbuf("result_grouped%d" % a, [P, P, PACK], BF16)
-            for first, count, bank_tag in parts[a]:
-                bank = ps.tile([P, count, P], F32, name="out_bank", tag=bank_tag)
-                for e in range(count):
-                    j = first + e
-                    codes, scales = val_mx[j // 2]
-                    features = slice(j % 2 * P, (j % 2 + 1) * P)
+        result_grouped = [sbuf("result_grouped%d" % a, [P, P, PACK], BF16) for a in range(Q_TILES)]
+        out_tags = (("bank_out", "bank_score1"), ("bank_score0", "bank_val0"))
+        for pair in range(2):
+            for a in range(Q_TILES):
+                cols = slice(a * P, (a + 1) * P)
+                bank = ps.tile([P, 2, P], F32, name="out_bank", tag=out_tags[pair][a])
+                for e in range(2):
+                    codes, scales = val_mx[2 * pair + e]
                     nc.tensor.matmul_mx(
                         out=bank[:, e, :],
-                        lhsT=codes[:, features].bitcast(FP8X4),
-                        lhsT_scale=scales[:, features],
+                        lhsT=codes.bitcast(FP8X4),
+                        lhsT_scale=scales,
                         rhs=weight_codes[:, cols].bitcast(FP8X4),
                         rhs_scale=weight_scales[:, cols],
                         start=True,
                         stop=True,
                     )
-                result = sbuf("result%d_%d" % (a, first), [P, count, P], F32)
+                result = sbuf("result%d_%d" % (pair, a), [P, 2, P], F32)
                 nc.scalar.copy(result[:], bank[:])
-                nc.sync.dma_start(out_rows[:, first : first + count, cols], result[:])
-                interleave(nc.vector.tensor_copy, result_grouped, first, result[:])
+                nc.sync.dma_start(out_rows[:, 2 * pair : 2 * pair + 2, cols], result[:])
+                interleave(nc.vector.tensor_copy, result_grouped[a], 2 * pair, result[:])
+        for a in range(Q_TILES):
+            cols = slice(a * P, (a + 1) * P)
             nc.vector.quantize_mx(
                 out=out_codes[:, cols].bitcast(FP8X4),
                 scales=out_scales[:, cols],
-                in_=result_grouped[:].rearrange("p c t -> p (c t)"),
+                in_=result_grouped[a][:].rearrange("p c t -> p (c t)"),
             )
         nc.sync.dma_start(out_1[0].rearrange("p c r -> p (c r)").bitcast(I32), out_codes[:].bitcast(I32))
         for quad in range(4):

@@ -3,7 +3,7 @@ from contextlib import ExitStack
 import concourse.mybir as mybir
 from concourse.masks import make_identity
 
-D, T, U, I, Q, E = 512, 1024, 1024, 512, 256, 512
+D, I, Q, E = 512, 512, 256, 512
 FLOPS = 2 * D * I * Q + 2 * I * E * Q
 
 F32 = mybir.dt.float32
@@ -19,9 +19,14 @@ AXIS_X = mybir.AxisListType.X
 
 P = 128
 PACK = 4
+PAIR = 2
+PER_COLUMN = 16
+LINE = 4
+QUADRANT = 32
 HALF = I // 2
-LIST_COLS = I // 16
 Q_TILES = Q // P
+LAST = PACK - 1
+LAST_ON_VECTOR = I // 4
 
 
 def tile_attend_compositeslots_pl_kernel(tc, query, keys, bkeys, size, vals, offs, offs2, out_0, out_1, out_2):
@@ -34,40 +39,63 @@ def tile_attend_compositeslots_pl_kernel(tc, query, keys, bkeys, size, vals, off
         def sbuf(name, shape, dtype, tag=None):
             return sb.tile(shape, dtype, name=name, tag=tag or name, align_bytes=64)
 
-        def quantise(name, grouped, width, tag=None):
-            codes = sbuf(name + "_codes", [P, width], U32, tag)
-            scales = sbuf(name + "_scales", [P, width], U8)
-            nc.vector.quantize_mx(out=codes[:].bitcast(FP8X4), scales=scales[:], in_=grouped[:].rearrange("p c t -> p (c t)"))
-            return codes, scales
+        def mx_tiles(name, width, tag=None):
+            return sbuf(name + "_codes", [P, width], U32, tag), sbuf(name + "_scales", [P, width], U8)
 
-        def half_of(lists, h):
-            return lists[:, h * LIST_COLS // 2 : (h + 1) * LIST_COLS // 2]
+        def quantise(mx, cols, grouped):
+            codes, scales = mx
+            nc.vector.quantize_mx(
+                out=codes[:, cols].bitcast(FP8X4), scales=scales[:, cols], in_=grouped.rearrange("p c t -> p (c t)")
+            )
+
+        def product(out, stationary, stationary_cols, moving, moving_cols):
+            nc.tensor.matmul_mx(
+                out=out,
+                lhsT=stationary[0][:, stationary_cols].bitcast(FP8X4),
+                lhsT_scale=stationary[1][:, stationary_cols],
+                rhs=moving[0][:, moving_cols].bitcast(FP8X4),
+                rhs_scale=moving[1][:, moving_cols],
+                start=True,
+                stop=True,
+            )
+
+        def picked(plane, lists, slots):
+            return plane[:].indirect(lists[:, slots.start // PER_COLUMN : slots.stop // PER_COLUMN])
 
         def interleave(copy, grouped, first, planes):
             count = planes.shape[1]
             copy(
-                grouped[:, :, first : first + count].rearrange("p (c i) t -> p c t i", i=4),
-                planes.rearrange("p t (c i) -> p c t i", i=4),
+                grouped[:, :, first : first + count].rearrange("p (c i) t -> p c t i", i=LINE),
+                planes.rearrange("p t (c i) -> p c t i", i=LINE),
             )
+
+        def group_words(copy, grouped, bank):
+            words = grouped.rearrange("p c t -> p (c t)").bitcast(F32).rearrange("p (c u) -> p c u", u=PAIR)
+            copy(words, bank[:].rearrange("p u c -> p c u"))
+
+        all_slots = slice(0, I)
+        halves = [slice(0, HALF), slice(HALF, I)]
+        q_cols = [slice(a * P, (a + 1) * P) for a in range(Q_TILES)]
+        one_tile = slice(0, P)
 
         size_sb = sbuf("size_sb", [P, PACK], F32)
         nc.sync.dma_start(size_sb[:], size.rearrange("o (p t) -> p (o t)", t=PACK))
         query_sb = sbuf("query_sb", [P, PACK, Q], F32)
         nc.sync.dma_start(query_sb[:], query.rearrange("(p t) q -> p t q", t=PACK))
-        own_lists = sbuf("own_lists", [P, LIST_COLS], U16)
-        shared_list = sbuf("shared_list", [P, LIST_COLS], U16)
+        own_lists = sbuf("own_lists", [P, I // PER_COLUMN], U16)
+        shared_list = sbuf("shared_list", [P, I // PER_COLUMN], U16)
 
         def load_plane(name, table, t):
             plane = sbuf(name + str(t), [P, table.shape[1]], F32)
             nc.sync.dma_start(plane[:], table.rearrange("(p t) n -> p t n", t=PACK)[:, t, :])
             return plane
 
-        base_planes, key_planes = [], []
-        for t in range(PACK):
+        base_planes = [load_plane("base_plane", bkeys, 0)]
+        nc.sync.dma_start(shared_list[:], offs2)
+        nc.sync.dma_start(own_lists[:], offs)
+        key_planes = [load_plane("key_plane", keys, 0)]
+        for t in range(1, PACK):
             base_planes.append(load_plane("base_plane", bkeys, t))
-            if t == 0:
-                nc.sync.dma_start(shared_list[:], offs2)
-                nc.sync.dma_start(own_lists[:], offs)
             key_planes.append(load_plane("key_plane", keys, t))
         val_planes = [load_plane("val_plane", vals, j) for j in range(PACK)]
 
@@ -76,7 +104,8 @@ def tile_attend_compositeslots_pl_kernel(tc, query, keys, bkeys, size, vals, off
 
         query_grouped = sbuf("query_grouped", [P, Q, PACK], BF16)
         interleave(nc.vector.tensor_copy, query_grouped, 0, query_sb[:])
-        query_codes, query_scales = quantise("query", query_grouped, Q)
+        query_mx = mx_tiles("query", Q)
+        quantise(query_mx, slice(0, Q), query_grouped[:])
 
         size_bank = ps.tile([P, PACK, P], F32, name="size_bank", tag="bank_size")
         size_spread = sbuf("size_spread", [P, PACK, P], F32)
@@ -84,96 +113,77 @@ def tile_attend_compositeslots_pl_kernel(tc, query, keys, bkeys, size, vals, off
         for t in range(PACK):
             nc.tensor.transpose(size_bank[:, t, :], size_spread[:, t, :], ident[:])
         size_row = sbuf("size_row", [P, I], F32)
-        nc.vector.tensor_copy(size_row[:].rearrange("p (u s e) -> p u s e", u=2, e=2), size_bank[:].rearrange("p (u e) s -> p u s e", u=2))
+        nc.vector.tensor_copy(
+            size_row[:].rearrange("p (u s e) -> p u s e", u=PAIR, e=PAIR),
+            size_bank[:].rearrange("p (u e) s -> p u s e", u=PAIR),
+        )
 
         base_picked = [sbuf("base_picked%d" % t, [P, I], F32) for t in range(PACK)]
-        km_low = sbuf("km_low", [P, 2, I], F32)
-        km_high = [sbuf("km_high%d" % h, [P, 2, HALF], F32) for h in range(2)]
+        km_low = sbuf("km_low", [P, PAIR, I], F32)
+        km_high = [sbuf("km_high%d" % h, [P, PAIR, HALF], F32) for h in range(2)]
         shared_bytes = sbuf("shared_bytes", [P, HALF + HALF * PACK], BF16)
         km_grouped = [
             sbuf("km_grouped0", [P, HALF, PACK], BF16)[:],
             shared_bytes[:, HALF:].rearrange("p (c t) -> p c t", t=PACK),
         ]
 
-        def gather_add(out, t, offsets, cols):
-            nc.vector.tensor_tensor(out, key_planes[t][:].indirect(offsets), base_picked[t][:, cols], ALU.add)
+        def gather_base(t, slots):
+            nc.scalar.activation(base_picked[t][:, slots], picked(base_planes[t], shared_list, slots), ACT.Copy)
 
-        halves = [slice(0, HALF), slice(HALF, I)]
-        last = PACK - 1
-        for t in range(last):
-            nc.scalar.activation(base_picked[t][:], base_planes[t][:].indirect(shared_list[:]), ACT.Copy)
-            if t < 2:
-                gather_add(km_low[:, t, :], t, own_lists[:], slice(0, I))
-            if t == 1:
-                for h in range(2):
-                    interleave(nc.vector.tensor_copy, km_grouped[h], 0, km_low[:, :, halves[h]])
-            if t == 2:
-                for h in range(2):
-                    gather_add(km_high[h][:, 0, :], t, half_of(own_lists, h), halves[h])
-        nc.scalar.activation(base_picked[last][:, halves[0]], base_planes[last][:].indirect(half_of(shared_list, 0)), ACT.Copy)
-        nc.vector.tensor_copy(base_picked[last][:, halves[1]], base_planes[last][:].indirect(half_of(shared_list, 1)))
+        def gather_add(out, t, slots):
+            nc.vector.tensor_tensor(out, picked(key_planes[t], own_lists, slots), base_picked[t][:, slots], ALU.add)
+
+        for t in range(PAIR):
+            gather_base(t, all_slots)
+            gather_add(km_low[:, t, :], t, all_slots)
+        for h in range(2):
+            interleave(nc.vector.tensor_copy, km_grouped[h], 0, km_low[:, :, halves[h]])
+        gather_base(PAIR, all_slots)
+        for h in range(2):
+            gather_add(km_high[h][:, 0, :], PAIR, halves[h])
+        gather_base(LAST, halves[0])
+        nc.vector.tensor_copy(base_picked[LAST][:, halves[1]], picked(base_planes[LAST], shared_list, halves[1]))
         key_picked = sbuf("key_picked", [P, HALF], F32)
-        gather_add(km_high[0][:, 1, :], last, half_of(own_lists, 0), halves[0])
-        nc.scalar.activation(key_picked[:], key_planes[last][:].indirect(half_of(own_lists, 1)), ACT.Copy)
-        nc.vector.tensor_tensor(km_high[1][:, 1, :], key_picked[:], base_picked[last][:, halves[1]], ALU.add)
-        interleave(nc.scalar.copy, km_grouped[0], 2, km_high[0][:])
-        interleave(nc.vector.tensor_copy, km_grouped[1], 2, km_high[1][:])
+        gather_add(km_high[0][:, 1, :], LAST, halves[0])
+        nc.scalar.activation(key_picked[:], picked(key_planes[LAST], own_lists, halves[1]), ACT.Copy)
+        nc.vector.tensor_tensor(km_high[1][:, 1, :], key_picked[:], base_picked[LAST][:, halves[1]], ALU.add)
+        interleave(nc.scalar.copy, km_grouped[0], PAIR, km_high[0][:])
+        interleave(nc.vector.tensor_copy, km_grouped[1], PAIR, km_high[1][:])
 
         score_banks = [ps.tile([P, I], F32, name="score_bank", tag="bank_score%d" % a) for a in range(Q_TILES)]
-        km_codes = sbuf("km_codes", [P, I], U32)
-        km_scales = sbuf("km_scales", [P, I], U8)
-
-        def scores(a, slots):
-            rows = slice(a * P, (a + 1) * P)
-            nc.tensor.matmul_mx(
-                out=score_banks[a][:, slots],
-                lhsT=query_codes[:, rows].bitcast(FP8X4),
-                lhsT_scale=query_scales[:, rows],
-                rhs=km_codes[:, slots].bitcast(FP8X4),
-                rhs_scale=km_scales[:, slots],
-                start=True,
-                stop=True,
-            )
-
+        km_mx = mx_tiles("km", I)
         for h in range(2):
-            nc.vector.quantize_mx(
-                out=km_codes[:, halves[h]].bitcast(FP8X4),
-                scales=km_scales[:, halves[h]],
-                in_=km_grouped[h].rearrange("p c t -> p (c t)"),
-            )
-            scores(0, halves[h])
-        scores(1, slice(0, I))
+            quantise(km_mx, halves[h], km_grouped[h])
+            product(score_banks[0][:, halves[h]], query_mx, q_cols[0], km_mx, halves[h])
+        product(score_banks[1][:], query_mx, q_cols[1], km_mx, all_slots)
 
-        def as_word_pairs(grouped):
-            return grouped.rearrange("p c t -> p (c t)").bitcast(F32).rearrange("p (c u) -> p c u", u=2)
+        val_picked = [
+            shared_bytes[:, 0:I],
+            sbuf("val_picked1", [P, I], BF16)[:],
+            shared_bytes[:, HALF : HALF + I],
+            sbuf("val_picked3", [P, I], BF16)[:],
+        ]
 
-        val_picked = {0: shared_bytes[:, 0:I], 1: sbuf("val_picked1", [P, I], BF16)[:], 3: sbuf("val_picked3", [P, I], BF16)[:]}
+        def gather_vals_scalar(j, slots):
+            nc.scalar.activation(val_picked[j][:, slots], picked(val_planes[j], shared_list, slots), ACT.Copy)
 
-        def gather_vals_scalar(j, cols, offsets):
-            nc.scalar.activation(val_picked[j][:, cols], val_planes[j][:].indirect(offsets), ACT.Copy)
-
-        def gather_vals_vector(j, cols, offsets):
-            nc.vector.tensor_copy(val_picked[j][:, cols], val_planes[j][:].indirect(offsets))
-
-        def slots(first, stop):
-            return slice(first, stop), shared_list[:, first // 16 : stop // 16]
-
-        val_banks = {}
+        def gather_vals_vector(j, slots):
+            nc.vector.tensor_copy(val_picked[j][:, slots], picked(val_planes[j], shared_list, slots))
 
         def turn_vals(j, bank_tag):
-            val_banks[j] = ps.tile([P, 2, P], F32, name="val_bank", tag=bank_tag)
+            bank = ps.tile([P, PAIR, P], F32, name="val_bank", tag=bank_tag)
             words = val_picked[j].bitcast(F32)
-            for u in range(2):
-                nc.tensor.transpose(val_banks[j][:, u, :], words[:, u : I // 2 : 2], ident[:])
+            for u in range(PAIR):
+                nc.tensor.transpose(bank[:, u, :], words[:, u : I // PAIR : PAIR], ident[:])
+            return bank
 
-        gather_vals_scalar(0, halves[0], half_of(shared_list, 0))
-        gather_vals_vector(0, halves[1], half_of(shared_list, 1))
-        gather_vals_scalar(1, slice(0, I), shared_list[:])
-        turn_vals(0, "bank_val0")
-        val_picked[2] = shared_bytes[:, HALF : HALF + I]
-        gather_vals_scalar(2, *slots(HALF, I))
+        gather_vals_scalar(0, halves[0])
+        gather_vals_vector(0, halves[1])
+        gather_vals_scalar(1, all_slots)
+        val_bank0 = turn_vals(0, "bank_val0")
+        gather_vals_scalar(2, halves[1])
 
-        neg_max = [val_picked[3][:, 0:2].bitcast(F32), val_picked[3][:, I - 2 : I].bitcast(F32)]
+        neg_max = [val_picked[LAST][:, 0:PAIR].bitcast(F32), val_picked[LAST][:, I - PAIR : I].bitcast(F32)]
         inv_sum = [sbuf("inv_sum%d" % a, [P, 1], F32) for a in range(Q_TILES)]
         row_sum = [sbuf("row_sum%d" % a, [P, 1], F32) for a in range(Q_TILES)]
         probs = [sbuf("probs%d" % a, [P, I], F32) for a in range(Q_TILES)]
@@ -182,114 +192,87 @@ def tile_attend_compositeslots_pl_kernel(tc, query, keys, bkeys, size, vals, off
             nc.vector.tensor_reduce(neg_max[a], score_banks[a][:], AXIS_X, ALU.max, negate=True)
         for a in range(Q_TILES):
             nc.scalar.activation(
-                probs[a][:].rearrange("p (u s e) -> p u s e", u=2, e=2),
-                score_banks[a][:].rearrange("p (s u e) -> p u s e", u=2, e=2),
+                probs[a][:].rearrange("p (u s e) -> p u s e", u=PAIR, e=PAIR),
+                score_banks[a][:].rearrange("p (s u e) -> p u s e", u=PAIR, e=PAIR),
                 ACT.Exp,
                 bias=neg_max[a],
                 accum_out=row_sum[a][:],
             )
-        gather_vals_vector(2, *slots(0, HALF))
-        gather_vals_vector(3, *slots(0, P))
-        gather_vals_scalar(3, *slots(P, I))
+        gather_vals_vector(2, halves[0])
+        gather_vals_vector(LAST, slice(0, LAST_ON_VECTOR))
+        gather_vals_scalar(LAST, slice(LAST_ON_VECTOR, I))
 
-        weight_codes = sbuf("weight_codes", [P, Q], U32)
-        weight_scales = sbuf("weight_scales", [P, Q], U8)
-        val_grouped, val_mx, weight_grouped, weight_banks = {}, {}, {}, {}
+        weight_mx = mx_tiles("weight", Q)
+        weight_banks = [ps.tile([P, PAIR, P], F32, name="weight_bank", tag="bank_weight%d" % a) for a in range(Q_TILES)]
+        sizes = [
+            [size_bank[:, PAIR * u : PAIR * (u + 1), :].rearrange("p e s -> p s e") for u in range(PAIR)],
+            [size_row[:, halves[u]].rearrange("p (s e) -> p s e", e=PAIR) for u in range(PAIR)],
+        ]
 
         def make_weights(a, u):
-            if a == 0:
-                sizes = size_bank[:, 2 * u : 2 * u + 2, :].rearrange("p e s -> p s e")
-            else:
-                sizes = size_row[:, halves[u]].rearrange("p (s e) -> p s e", e=2)
             nc.vector.scalar_tensor_tensor(
-                weights[a][:, halves[u]].rearrange("p (s e) -> p s e", e=2),
-                probs[a][:, halves[u]].rearrange("p (s e) -> p s e", e=2),
+                weights[a][:, halves[u]].rearrange("p (s e) -> p s e", e=PAIR),
+                probs[a][:, halves[u]].rearrange("p (s e) -> p s e", e=PAIR),
                 inv_sum[a][:],
-                sizes,
+                sizes[a][u],
                 ALU.mult,
                 ALU.mult,
             )
             nc.tensor.transpose(weight_banks[a][:, u, :], weights[a][:, halves[u]].bitcast(F32), ident[:])
 
-        def group_vals(j, copy, grouped):
-            copy(as_word_pairs(grouped), val_banks[j][:].rearrange("p u c -> p c u"))
-
         def group_weights(a):
-            weight_grouped[a] = sbuf("weight_grouped%d" % a, [P, P, PACK], BF16)
-            nc.scalar.copy(as_word_pairs(weight_grouped[a][:]), weight_banks[a][:].rearrange("p u c -> p c u"))
+            grouped = sbuf("weight_grouped%d" % a, [P, P, PACK], BF16)
+            group_words(nc.scalar.copy, grouped[:], weight_banks[a])
+            return grouped
 
-        def quantise_weights(a):
-            cols = slice(a * P, (a + 1) * P)
-            nc.vector.quantize_mx(
-                out=weight_codes[:, cols].bitcast(FP8X4),
-                scales=weight_scales[:, cols],
-                in_=weight_grouped[a][:].rearrange("p c t -> p (c t)"),
-            )
-
-        for a in range(Q_TILES):
-            weight_banks[a] = ps.tile([P, 2, P], F32, name="weight_bank", tag="bank_weight%d" % a)
         nc.vector.reciprocal(inv_sum[0][:], row_sum[0][:])
         make_weights(0, 0)
         nc.vector.reciprocal(inv_sum[1][:], row_sum[1][:])
         make_weights(0, 1)
-        group_weights(0)
+        weight_grouped = [group_weights(0)]
         make_weights(1, 0)
         make_weights(1, 1)
-        group_weights(1)
+        weight_grouped.append(group_weights(1))
 
-        low_grouped = sbuf("val_grouped01", [P, 2 * P, PACK], BF16, "probs1")
-        group_vals(0, nc.vector.tensor_copy, low_grouped[:, 0:P, :])
-        turn_vals(1, "bank_score0")
-        group_vals(1, nc.vector.tensor_copy, low_grouped[:, P:, :])
-        for j, bank_tag, tag in ((2, "bank_val2", "row_sum1"), (3, "bank_size", None)):
-            turn_vals(j, bank_tag)
-            val_grouped[j] = sbuf("val_grouped%d" % j, [P, P, PACK], BF16, tag)
-            group_vals(j, nc.scalar.copy, val_grouped[j][:])
-        quantise_weights(0)
-        low_codes, low_scales = quantise("val01", low_grouped, 2 * P)
-        for j in range(2):
-            val_mx[j] = low_codes[:, j * P : (j + 1) * P], low_scales[:, j * P : (j + 1) * P]
-        codes, scales = quantise("val2", val_grouped[2], P, "size_row")
-        val_mx[2] = codes[:], scales[:]
-        quantise_weights(1)
-        codes, scales = quantise("val3", val_grouped[3], P)
-        val_mx[3] = codes[:], scales[:]
+        val_grouped = [
+            sbuf("val_grouped%d" % j, [P, P, PACK], BF16, tag) for j, tag in enumerate(("probs0", None, "row_sum1", None))
+        ]
+        group_words(nc.vector.tensor_copy, val_grouped[0][:], val_bank0)
+        for j, bank_tag in ((1, "bank_score0"), (2, "bank_val2"), (LAST, "bank_size")):
+            group_words(nc.scalar.copy, val_grouped[j][:], turn_vals(j, bank_tag))
+        val_mx = [mx_tiles("val%d" % j, P, tag) for j, tag in enumerate((None, None, "size_row", None))]
+        val_operand = [(mx, one_tile) for mx in val_mx]
+        for j in (1, 2, 0):
+            quantise(val_mx[j], one_tile, val_grouped[j][:])
+        for a in range(Q_TILES):
+            quantise(weight_mx, q_cols[a], weight_grouped[a][:])
+        quantise(val_mx[LAST], one_tile, val_grouped[LAST][:])
 
         out_rows = out_0.rearrange("(p j) q -> p j q", j=PACK)
-        out_codes = sbuf("out_codes", [P, Q], U32)
-        out_scales = sbuf("out_scales", [P, Q], U8)
+        out_mx = mx_tiles("out", Q)
         result_grouped = [sbuf("result_grouped%d" % a, [P, P, PACK], BF16) for a in range(Q_TILES)]
         out_tags = (("bank_out", "bank_score1"), ("bank_score0", "bank_val0"))
-        for pair in range(2):
+        for pair in range(PACK // PAIR):
+            first = PAIR * pair
             for a in range(Q_TILES):
-                cols = slice(a * P, (a + 1) * P)
-                bank = ps.tile([P, 2, P], F32, name="out_bank", tag=out_tags[pair][a])
-                for e in range(2):
-                    codes, scales = val_mx[2 * pair + e]
-                    nc.tensor.matmul_mx(
-                        out=bank[:, e, :],
-                        lhsT=codes.bitcast(FP8X4),
-                        lhsT_scale=scales,
-                        rhs=weight_codes[:, cols].bitcast(FP8X4),
-                        rhs_scale=weight_scales[:, cols],
-                        start=True,
-                        stop=True,
-                    )
-                result = sbuf("result%d_%d" % (pair, a), [P, 2, P], F32)
-                nc.scalar.copy(result[:], bank[:])
-                nc.sync.dma_start(out_rows[:, 2 * pair : 2 * pair + 2, cols], result[:])
-                interleave(nc.vector.tensor_copy, result_grouped[a], 2 * pair, result[:])
+                bank = ps.tile([P, PAIR, P], F32, name="out_bank", tag=out_tags[pair][a])
+                for e in range(PAIR):
+                    product(bank[:, e, :], *val_operand[first + e], weight_mx, q_cols[a])
+                result = sbuf("result%d_%d" % (pair, a), [P, PAIR, P], F32)
+                if first + PAIR == PACK and a == Q_TILES - 1:
+                    interleave(nc.vector.tensor_copy, result_grouped[a], first, bank[:])
+                    nc.scalar.copy(result[:], bank[:])
+                else:
+                    nc.scalar.copy(result[:], bank[:])
+                    interleave(nc.vector.tensor_copy, result_grouped[a], first, result[:])
+                nc.sync.dma_start(out_rows[:, first : first + PAIR, q_cols[a]], result[:])
         for a in range(Q_TILES):
-            cols = slice(a * P, (a + 1) * P)
-            nc.vector.quantize_mx(
-                out=out_codes[:, cols].bitcast(FP8X4),
-                scales=out_scales[:, cols],
-                in_=result_grouped[a][:].rearrange("p c t -> p (c t)"),
-            )
+            quantise(out_mx, q_cols[a], result_grouped[a][:])
+        out_codes, out_scales = out_mx
         nc.sync.dma_start(out_1[0].rearrange("p c r -> p (c r)").bitcast(I32), out_codes[:].bitcast(I32))
-        for quad in range(4):
+        for quad in range(P // QUADRANT):
             queue = nc.sync if quad % 2 else nc.scalar
             queue.dma_start(
-                out_2[0, 4 * quad : 4 * quad + 4, :].bitcast(I32),
-                out_scales[32 * quad : 32 * quad + 4, :].bitcast(I32),
+                out_2[0, PACK * quad : PACK * (quad + 1), :].bitcast(I32),
+                out_scales[QUADRANT * quad : QUADRANT * quad + PACK, :].bitcast(I32),
             )

from contextlib import ExitStack

import concourse.mybir as mybir
from concourse.masks import make_identity

D, I, Q, E = 512, 512, 256, 512
FLOPS = 2 * D * I * Q + 2 * I * E * Q

F32 = mybir.dt.float32
BF16 = mybir.dt.bfloat16
I32 = mybir.dt.int32
U32 = mybir.dt.uint32
U16 = mybir.dt.uint16
U8 = mybir.dt.uint8
FP8X4 = mybir.dt.float8_e4m3fn_x4
ACT = mybir.ActivationFunctionType
ALU = mybir.AluOpType
AXIS_X = mybir.AxisListType.X

P = 128
PACK = 4
PAIR = 2
PER_COLUMN = 16
LINE = 4
QUADRANT = 32
HALF = I // 2
Q_TILES = Q // P
LAST = PACK - 1
LAST_ON_VECTOR = I // 4


def tile_attend_compositeslots_pl_kernel(tc, query, keys, bkeys, size, vals, offs, offs2, out_0, out_1, out_2):
    nc = tc.nc

    with ExitStack() as ctx:
        sb = ctx.enter_context(tc.tile_pool(name="sb", bufs=1))
        ps = ctx.enter_context(tc.psum_pool(name="ps", bufs=1))

        def sbuf(name, shape, dtype, tag=None):
            return sb.tile(shape, dtype, name=name, tag=tag or name, align_bytes=64)

        def mx_tiles(name, width, tag=None):
            return sbuf(name + "_codes", [P, width], U32, tag), sbuf(name + "_scales", [P, width], U8)

        def quantise(mx, cols, grouped):
            codes, scales = mx
            nc.vector.quantize_mx(
                out=codes[:, cols].bitcast(FP8X4), scales=scales[:, cols], in_=grouped.rearrange("p c t -> p (c t)")
            )

        def product(out, stationary, stationary_cols, moving, moving_cols):
            nc.tensor.matmul_mx(
                out=out,
                lhsT=stationary[0][:, stationary_cols].bitcast(FP8X4),
                lhsT_scale=stationary[1][:, stationary_cols],
                rhs=moving[0][:, moving_cols].bitcast(FP8X4),
                rhs_scale=moving[1][:, moving_cols],
                start=True,
                stop=True,
            )

        def picked(plane, lists, slots):
            return plane[:].indirect(lists[:, slots.start // PER_COLUMN : slots.stop // PER_COLUMN])

        def interleave(copy, grouped, first, planes):
            count = planes.shape[1]
            copy(
                grouped[:, :, first : first + count].rearrange("p (c i) t -> p c t i", i=LINE),
                planes.rearrange("p t (c i) -> p c t i", i=LINE),
            )

        def group_words(copy, grouped, bank):
            words = grouped.rearrange("p c t -> p (c t)").bitcast(F32).rearrange("p (c u) -> p c u", u=PAIR)
            copy(words, bank[:].rearrange("p u c -> p c u"))

        all_slots = slice(0, I)
        halves = [slice(0, HALF), slice(HALF, I)]
        q_cols = [slice(a * P, (a + 1) * P) for a in range(Q_TILES)]
        one_tile = slice(0, P)

        size_sb = sbuf("size_sb", [P, PACK], F32)
        nc.sync.dma_start(size_sb[:], size.rearrange("o (p t) -> p (o t)", t=PACK))
        query_sb = sbuf("query_sb", [P, PACK, Q], F32)
        nc.sync.dma_start(query_sb[:], query.rearrange("(p t) q -> p t q", t=PACK))
        own_lists = sbuf("own_lists", [P, I // PER_COLUMN], U16)
        shared_list = sbuf("shared_list", [P, I // PER_COLUMN], U16)

        def load_plane(name, table, t):
            plane = sbuf(name + str(t), [P, table.shape[1]], F32)
            nc.sync.dma_start(plane[:], table.rearrange("(p t) n -> p t n", t=PACK)[:, t, :])
            return plane

        base_planes = [load_plane("base_plane", bkeys, 0)]
        nc.sync.dma_start(shared_list[:], offs2)
        nc.sync.dma_start(own_lists[:], offs)
        key_planes = [load_plane("key_plane", keys, 0)]
        for t in range(1, PACK):
            base_planes.append(load_plane("base_plane", bkeys, t))
            key_planes.append(load_plane("key_plane", keys, t))
        val_planes = [load_plane("val_plane", vals, j) for j in range(PACK)]

        ident = sbuf("ident", [P, P], F32)
        make_identity(nc, ident[:])

        query_grouped = sbuf("query_grouped", [P, Q, PACK], BF16)
        interleave(nc.vector.tensor_copy, query_grouped, 0, query_sb[:])
        query_mx = mx_tiles("query", Q)
        quantise(query_mx, slice(0, Q), query_grouped[:])

        size_bank = ps.tile([P, PACK, P], F32, name="size_bank", tag="bank_size")
        size_spread = sbuf("size_spread", [P, PACK, P], F32)
        nc.scalar.activation(size_spread[:], size_sb[:].unsqueeze(2).to_broadcast([P, PACK, P]), ACT.Copy)
        for t in range(PACK):
            nc.tensor.transpose(size_bank[:, t, :], size_spread[:, t, :], ident[:])
        size_row = sbuf("size_row", [P, I], F32)
        nc.vector.tensor_copy(
            size_row[:].rearrange("p (u s e) -> p u s e", u=PAIR, e=PAIR),
            size_bank[:].rearrange("p (u e) s -> p u s e", u=PAIR),
        )

        base_picked = [sbuf("base_picked%d" % t, [P, I], F32) for t in range(PACK)]
        km_low = sbuf("km_low", [P, PAIR, I], F32)
        km_high = [sbuf("km_high%d" % h, [P, PAIR, HALF], F32) for h in range(2)]
        shared_bytes = sbuf("shared_bytes", [P, HALF + HALF * PACK], BF16)
        km_grouped = [
            sbuf("km_grouped0", [P, HALF, PACK], BF16)[:],
            shared_bytes[:, HALF:].rearrange("p (c t) -> p c t", t=PACK),
        ]

        def gather_base(t, slots):
            nc.scalar.activation(base_picked[t][:, slots], picked(base_planes[t], shared_list, slots), ACT.Copy)

        def gather_add(out, t, slots):
            nc.vector.tensor_tensor(out, picked(key_planes[t], own_lists, slots), base_picked[t][:, slots], ALU.add)

        for t in range(PAIR):
            gather_base(t, all_slots)
            gather_add(km_low[:, t, :], t, all_slots)
        for h in range(2):
            interleave(nc.vector.tensor_copy, km_grouped[h], 0, km_low[:, :, halves[h]])
        gather_base(PAIR, all_slots)
        for h in range(2):
            gather_add(km_high[h][:, 0, :], PAIR, halves[h])
        gather_base(LAST, halves[0])
        nc.vector.tensor_copy(base_picked[LAST][:, halves[1]], picked(base_planes[LAST], shared_list, halves[1]))
        key_picked = sbuf("key_picked", [P, HALF], F32)
        gather_add(km_high[0][:, 1, :], LAST, halves[0])
        nc.scalar.activation(key_picked[:], picked(key_planes[LAST], own_lists, halves[1]), ACT.Copy)
        nc.vector.tensor_tensor(km_high[1][:, 1, :], key_picked[:], base_picked[LAST][:, halves[1]], ALU.add)
        interleave(nc.scalar.copy, km_grouped[0], PAIR, km_high[0][:])
        interleave(nc.vector.tensor_copy, km_grouped[1], PAIR, km_high[1][:])

        score_banks = [ps.tile([P, I], F32, name="score_bank", tag="bank_score%d" % a) for a in range(Q_TILES)]
        km_mx = mx_tiles("km", I)
        for h in range(2):
            quantise(km_mx, halves[h], km_grouped[h])
            product(score_banks[0][:, halves[h]], query_mx, q_cols[0], km_mx, halves[h])
        product(score_banks[1][:], query_mx, q_cols[1], km_mx, all_slots)

        val_picked = [
            shared_bytes[:, 0:I],
            sbuf("val_picked1", [P, I], BF16)[:],
            shared_bytes[:, HALF : HALF + I],
            sbuf("val_picked3", [P, I], BF16)[:],
        ]

        def gather_vals_scalar(j, slots):
            nc.scalar.activation(val_picked[j][:, slots], picked(val_planes[j], shared_list, slots), ACT.Copy)

        def gather_vals_vector(j, slots):
            nc.vector.tensor_copy(val_picked[j][:, slots], picked(val_planes[j], shared_list, slots))

        def turn_vals(j, bank_tag):
            bank = ps.tile([P, PAIR, P], F32, name="val_bank", tag=bank_tag)
            words = val_picked[j].bitcast(F32)
            for u in range(PAIR):
                nc.tensor.transpose(bank[:, u, :], words[:, u : I // PAIR : PAIR], ident[:])
            return bank

        gather_vals_scalar(0, halves[0])
        gather_vals_vector(0, halves[1])
        gather_vals_scalar(1, all_slots)
        val_bank0 = turn_vals(0, "bank_val0")
        gather_vals_scalar(2, halves[1])

        neg_max = [val_picked[LAST][:, 0:PAIR].bitcast(F32), val_picked[LAST][:, I - PAIR : I].bitcast(F32)]
        inv_sum = [sbuf("inv_sum%d" % a, [P, 1], F32) for a in range(Q_TILES)]
        row_sum = [sbuf("row_sum%d" % a, [P, 1], F32) for a in range(Q_TILES)]
        probs = [sbuf("probs%d" % a, [P, I], F32) for a in range(Q_TILES)]
        weights = [sbuf("weights%d" % a, [P, I], BF16) for a in range(Q_TILES)]
        for a in range(Q_TILES):
            nc.vector.tensor_reduce(neg_max[a], score_banks[a][:], AXIS_X, ALU.max, negate=True)
        for a in range(Q_TILES):
            nc.scalar.activation(
                probs[a][:].rearrange("p (u s e) -> p u s e", u=PAIR, e=PAIR),
                score_banks[a][:].rearrange("p (s u e) -> p u s e", u=PAIR, e=PAIR),
                ACT.Exp,
                bias=neg_max[a],
                accum_out=row_sum[a][:],
            )
        gather_vals_vector(2, halves[0])
        gather_vals_vector(LAST, slice(0, LAST_ON_VECTOR))
        gather_vals_scalar(LAST, slice(LAST_ON_VECTOR, I))

        weight_mx = mx_tiles("weight", Q)
        weight_banks = [ps.tile([P, PAIR, P], F32, name="weight_bank", tag="bank_weight%d" % a) for a in range(Q_TILES)]
        sizes = [
            [size_bank[:, PAIR * u : PAIR * (u + 1), :].rearrange("p e s -> p s e") for u in range(PAIR)],
            [size_row[:, halves[u]].rearrange("p (s e) -> p s e", e=PAIR) for u in range(PAIR)],
        ]

        def make_weights(a, u):
            nc.vector.scalar_tensor_tensor(
                weights[a][:, halves[u]].rearrange("p (s e) -> p s e", e=PAIR),
                probs[a][:, halves[u]].rearrange("p (s e) -> p s e", e=PAIR),
                inv_sum[a][:],
                sizes[a][u],
                ALU.mult,
                ALU.mult,
            )
            nc.tensor.transpose(weight_banks[a][:, u, :], weights[a][:, halves[u]].bitcast(F32), ident[:])

        def group_weights(a):
            grouped = sbuf("weight_grouped%d" % a, [P, P, PACK], BF16)
            group_words(nc.scalar.copy, grouped[:], weight_banks[a])
            return grouped

        nc.vector.reciprocal(inv_sum[0][:], row_sum[0][:])
        make_weights(0, 0)
        nc.vector.reciprocal(inv_sum[1][:], row_sum[1][:])
        make_weights(0, 1)
        weight_grouped = [group_weights(0)]
        make_weights(1, 0)
        make_weights(1, 1)
        weight_grouped.append(group_weights(1))

        val_grouped = [
            sbuf("val_grouped%d" % j, [P, P, PACK], BF16, tag) for j, tag in enumerate(("probs0", None, "row_sum1", None))
        ]
        group_words(nc.vector.tensor_copy, val_grouped[0][:], val_bank0)
        for j, bank_tag in ((1, "bank_score0"), (2, "bank_val2"), (LAST, "bank_size")):
            group_words(nc.scalar.copy, val_grouped[j][:], turn_vals(j, bank_tag))
        val_mx = [mx_tiles("val%d" % j, P, tag) for j, tag in enumerate((None, None, "size_row", None))]
        val_operand = [(mx, one_tile) for mx in val_mx]
        for j in (1, 2, 0):
            quantise(val_mx[j], one_tile, val_grouped[j][:])
        for a in range(Q_TILES):
            quantise(weight_mx, q_cols[a], weight_grouped[a][:])
        quantise(val_mx[LAST], one_tile, val_grouped[LAST][:])

        out_rows = out_0.rearrange("(p j) q -> p j q", j=PACK)
        out_mx = mx_tiles("out", Q)
        result_grouped = [sbuf("result_grouped%d" % a, [P, P, PACK], BF16) for a in range(Q_TILES)]
        out_tags = (("bank_out", "bank_score1"), ("bank_score0", "bank_val0"))
        for pair in range(PACK // PAIR):
            first = PAIR * pair
            for a in range(Q_TILES):
                bank = ps.tile([P, PAIR, P], F32, name="out_bank", tag=out_tags[pair][a])
                for e in range(PAIR):
                    product(bank[:, e, :], *val_operand[first + e], weight_mx, q_cols[a])
                result = sbuf("result%d_%d" % (pair, a), [P, PAIR, P], F32)
                if first + PAIR == PACK and a == Q_TILES - 1:
                    interleave(nc.vector.tensor_copy, result_grouped[a], first, bank[:])
                    nc.scalar.copy(result[:], bank[:])
                else:
                    nc.scalar.copy(result[:], bank[:])
                    interleave(nc.vector.tensor_copy, result_grouped[a], first, result[:])
                nc.sync.dma_start(out_rows[:, first : first + PAIR, q_cols[a]], result[:])
        for a in range(Q_TILES):
            quantise(out_mx, q_cols[a], result_grouped[a][:])
        out_codes, out_scales = out_mx
        nc.sync.dma_start(out_1[0].rearrange("p c r -> p (c r)").bitcast(I32), out_codes[:].bitcast(I32))
        for quad in range(P // QUADRANT):
            queue = nc.sync if quad % 2 else nc.scalar
            queue.dma_start(
                out_2[0, PACK * quad : PACK * (quad + 1), :].bitcast(I32),
                out_scales[QUADRANT * quad : QUADRANT * quad + PACK, :].bitcast(I32),
            )
